import numpy as np, ml_dtypes
CORES = [6,15,38,47]
N = 4
import mx_ref
BF = ml_dtypes.bfloat16
def gentries(a):
    return np.ascontiguousarray(a.reshape(8, 16, -1).transpose(0, 2, 1)).reshape(8, -1)
def gtable(e):
    e = np.asarray(e); return np.ascontiguousarray(e.reshape(8, -1, 16).transpose(0, 2, 1)).reshape(128, -1).astype(np.int32)
def gcols(t, e):
    v = np.concatenate([t.reshape(8, 16, -1, 4), np.zeros((8, 16, 1, 4), BF)], axis=2)
    return np.ascontiguousarray(np.stack([v[g][:, e[g]] for g in range(8)])).reshape(128, -1)
def tile(rs):
    return np.stack(rs, axis=2).reshape(128, -1).astype(BF)
def pick(q, e):
    c = np.concatenate([q[0].reshape(128, -1, 4), np.zeros((128, 1, 4), np.uint8)], axis=1); s = np.concatenate([q[1], np.ones((16, 1), np.uint8)], axis=1)
    return (np.ascontiguousarray(c[:, e].reshape(128, -1)), np.ascontiguousarray(s[:, e]))
def join(*qs):
    return (np.concatenate([q[0] for q in qs], axis=1), np.concatenate([q[1] for q in qs], axis=1))
def put(q, e, v):
    c, s = q[0].reshape(128, -1, 4).copy(), q[1].copy(); c[:, e] = v[0].reshape(128, -1, 4); s[:, e] = v[1]
    return (c.reshape(128, -1), s)
def pk(c, s):
    return (np.ascontiguousarray(c), mx_ref.live(s))
def emit(q):
    return q[0], q[1]
def packed(v, rng):
    q = [mx_ref.quantize(np.ascontiguousarray(v[r])) for r in range(N)]
    return np.stack([a for a, b in q]), np.stack([mx_ref.plane(b, rng) for a, b in q])
def values_of_codes():
    e, c = np.zeros((128, 128, 4), np.float32), np.zeros((128, 2, 4), np.uint8)
    e[np.arange(128), np.arange(128), 0] = 1
    c[:127, :, 0] = np.arange(256).reshape(2, 128).T[:127]
    return mx_ref.matmul(mx_ref.quantize(e.reshape(128, 512).astype(BF)), (c.reshape(128, 8), np.full((16, 2), 127, np.uint8))).T.reshape(-1).astype(np.float64)
CODE_VALUE, SCALE_VALUE = values_of_codes(), 2.0 ** (np.arange(256) - 127.0)
def decode(q):
    return (CODE_VALUE[q[0]].reshape(16, 8, -1, 4) * SCALE_VALUE[q[1]][:, None, :, None] + 0.0).reshape(128, -1).astype(np.float32)
def f(rng, *shape):
    return mx_ref.flush((rng.standard_normal(shape, dtype=np.float32) * np.exp2(rng.integers(-2, 3, shape[:-1] + (1,)))).astype(BF))
def wide(rng, *shape, cols=0):
    v = rng.standard_normal(shape, dtype=np.float32) * np.exp2(rng.integers(-12, 13, shape)).astype(np.float32)
    if cols: v *= np.repeat(np.exp2(rng.integers(-cols, cols + 1, shape[:-2] + (1, shape[-1] // 4))) * (rng.random(shape[:-2] + (1, shape[-1] // 4)) > 0.0625), 4, axis=-1).astype(np.float32)
    return mx_ref.flush(v.astype(BF))
C, K = 384, 96
STRIDE = [1, 2, 3]
def at(t, e):
    return np.take_along_axis(t, e, axis=1)
def halved(a, b):
    return ((a.astype(np.float32) + b.astype(np.float32)) * np.float32(0.5)).astype(BF)
def big(v):
    v = np.array(v).astype(np.float32)
    v[np.abs(v) < np.float32(2.0 ** -16)] = 0
    return np.clip(v, -2.0 ** 21, 2.0 ** 21).astype(BF)
def numbers_of(rng):
    return {"x": big(f(rng, N, 128, 4 * C)), "u": np.array(f(rng, N, 128, 512)), "v": np.array(f(rng, N, 128, 512))}
def pairs(a, b):
    e = np.zeros(C, np.int64)
    e[a] = b
    e[b] = a
    return e
def pairing(rng):
    z = rng.permutation(C).reshape(2, -1)
    return pairs(z[0], z[1])
def pairings(rng):
    return np.stack([gtable(np.stack([pairing(rng) for g in range(8)])) for r in range(N)])
def layers(rng, still=[]):
    w = big(f(rng, N, 128, 2048).astype(np.float32) * np.float32(0.0625)).reshape(N, 8, 16, 4, 8, 16, 4)
    for i in still:
        w[:, :, i] = 0
        w[:, :, :, :, :, i] = 0
    return w
def weights(rng, w):
    c, s = packed(np.ascontiguousarray(w).reshape(N, 128, 2048), rng)
    return {"wc": c, "ws": s}
def setup_inputs(rng):
    return {**numbers_of(rng), "m": pairings(rng), **weights(rng, layers(rng))}
def setup_inputs_ties(rng):
    d = numbers_of(rng)
    x = d["x"].reshape(N, 8, 16, C, 4)
    x[:, :, 0] = 0
    x[:, :, 0, :, 0] = rng.integers(1, 4, (N, 8, C)).astype(np.float32).astype(BF)
    u = d["u"].reshape(N, 128, 128, 4)
    u[:, :, ::16] = 0
    o = rng.permutation(N)
    for r in range(N):
        for h in range(0, 128, 16): u[r, h, h, 0] = 0.0 if r == o[0] else -1.0 if r == o[1] else 1.0
    w = layers(rng, [0])
    a = 2 * int(rng.integers(N // 2))
    x[a, :, 8:] = 2.0 ** 18
    x[a + 1, :, 8:] = -2.0 ** 18
    w[a:a + 2, :, 8:] = 0
    return {"x": x.reshape(N, 128, 4 * C), "u": u.reshape(N, 128, 512), "v": d["v"], "m": pairings(rng), **weights(rng, w)}
def setup_inputs_near(rng):
    d = numbers_of(rng)
    x = d["x"].astype(np.float32).reshape(N, 8, 16, C, 4)
    x[:, :, 0] = 0
    x[:, :, 8:] = 0
    u = d["u"].reshape(N, 128, 128, 4)
    u[:, :, ::16] = 0
    s = rng.integers(0, 16, (N, 8, C))
    digits = ((s[:, :, :, None] >> np.arange(4)) & 1) * np.exp2(np.arange(4) - 23.0)
    o = rng.permutation(N) % 4
    for r in range(N):
        sign = rng.permutation(8) % 2 * 2.0 - 1.0
        k = 2.0 ** -4 if o[r] == 1 else 1.0
        c = 1.0 if o[r] == 0 else 2.0 ** -30
        if o[r] < 2:
            x[r, :, 0, :, 0] = k
            x[r, :, 11, :, 0] = k * 2.0 ** -10
        if o[r] < 3: x[r, :, 8] = k * digits[r]
        if o[r] == 2:
            for g in rng.permutation(8)[:4]:
                a = rng.permutation(C)
                x[r, g, 0, a[0], 0] = 2.0 ** 21
                x[r, g, 0, a[1], 0] = -2.0 ** 21
        if o[r] == 3:
            e = rng.integers(0, 2, (8, C))
            x[r, :, 9, :, 0] = e * 1.125 * 2.0 ** -27
            x[r, :, 10, :, 0] = (1 - e) * 2.0 ** -27
            x[r, :, 12, :, 0] = 2.0 ** -27
        for g in range(8):
            h = 16 * g
            if o[r] < 3:
                u[r, h, h, 0] = sign[g] * (c if o[r] < 2 else 2.0 ** 30)
                u[r, h + 8, h] = sign[g] * c
            if o[r] < 2: u[r, h + 11, h, 0] = sign[g] * c
            if o[r] == 3:
                u[r, h + 9, h, 0] = sign[g] * 1.125 * c
                u[r, h + 10, h, 0] = sign[g] * 1.25 * c
                u[r, h + 12, h, 0] = sign[g] * -1.125 * c
    return {"x": x.reshape(N, 128, 4 * C).astype(BF), "u": u.reshape(N, 128, 512), "v": d["v"], "m": pairings(rng), **weights(rng, layers(rng, [0, 8, 9, 10, 11, 12, 13, 14, 15]))}
def setup_inputs_blocks(rng):
    d = numbers_of(rng)
    k = rng.integers(-2, 3, (8, 1, 1, 1, 1))
    unit = np.exp2(k * 1.0).reshape(8, 1, 1, 1)
    e = np.arange(32).reshape(8, 1, 4)
    x = np.exp2(k - rng.integers(8, 15, (N, 8, 2, 8, C, 4))) * (1.0 + (2 * rng.integers(0, 64, (N, 8, 2, 8, C, 4)) + 1) * 2.0 ** -7)
    x[:, :, 0, 1, :, 0] = np.exp2(k.reshape(8, 1) - rng.integers(13, 15, (N, 8, C))) * (1.0 + (2 * rng.integers(0, 64, (N, 8, C)) + 1) * 2.0 ** -7)
    i = rng.integers(0, 31, (N, 8, 1, C, 1))
    i = np.where(i >= 4, i + 1, i)
    x[:, :, 0] = np.where(e == i, 1.96875 * unit, x[:, :, 0])
    x = x * (rng.integers(0, 2, x.shape) * 2.0 - 1.0)
    i = rng.integers(0, 32, (N, 8, 1, 1, 1))
    x[:, :, 1] = np.where(e == i, np.where(rng.random((N, 8, 1, C, 1)) < 0.5, 3.0, 0.9375) * unit, x[:, :, 1])
    m = np.stack([np.stack([pairing(rng) for g in range(8)]) for r in range(N)])
    for g in rng.permutation(8)[:4]:
        for a in range(0, N, 4):
            z = rng.permutation(C)
            t = np.roll(z, -1)
            m[a:a + 2, g] = pairs(z[::2], z[1::2])
            m[a + 2:a + 4, g] = pairs(t[::2], t[1::2])
            x[a:a + 4, g, 0, 1, :, 0] = -1.0
            x[a:a + 2, g, 0, 1, t[::4], 0] = 1.0
            x[a + 2:a + 4, g, 0, 1, z[::4], 0] = 1.0
    u = d["u"].reshape(N, 128, 128, 4)
    u[:, :, ::16] = 0
    for h in range(0, 128, 16): u[:, h + 1, h, 0] = 1.0
    w = layers(rng)
    w[:, :, :, :, :, 1] = 0
    w[:, :, :, :, :, 8:] = 0
    return {"x": x.astype(np.float32).reshape(N, 128, 4 * C).astype(BF), "u": u.reshape(N, 128, 512), "v": d["v"], "m": np.stack([gtable(m[r]) for r in range(N)]), **weights(rng, w)}
def setup_inputs_ends(rng):
    d = numbers_of(rng)
    v = np.array(d["v"]).astype(np.float32)
    u = d["u"].reshape(N, 128, 128, 4)
    u[:, :, ::16] = 0
    x = np.zeros((N, 8, 16, C, 4), np.float32)
    w = np.zeros((N, 128, 4, 128, 4), np.float32)
    m = np.zeros((N, 8, C), np.int64)
    high = rng.random((N, 8, C)) < 0.5
    kind = rng.permutation(N // 2)
    n = np.arange(128)
    for i in range(N // 2):
        a, b = 2 * i, 2 * i + 1
        for g in range(8):
            if kind[i] == 1:
                m[a, g] = np.arange(C)[::-1] if g % 2 else np.arange(C) ^ 1
                m[b, g] = m[a, g]
                continue
            z = rng.permutation(C).reshape(-1, 4 if kind[i] == 3 else C)
            t = np.roll(z, -1, axis=1)
            m[a, g] = pairs(z[:, ::2], z[:, 1::2])
            m[b, g] = pairs(t[:, ::2], t[:, 1::2])
            high[a, g] = False
            high[b, g] = False
            high[a, g, t[:, ::4]] = True
            high[b, g, z[:, ::4]] = True
        one = a + int(rng.integers(2))
        whole = rng.permutation(8)
        for r in (a, b):
            large = kind[i] == 2 or (kind[i] < 2 and r == one)
            below = kind[i] == 1 and r == one
            top = -1.0 if below else -0.5 if r == one and kind[i] in (0, 2) else 1.0
            x[r] = ((2.0 ** 21 if large else 2.0 ** -27) * np.where(high[r], top, -0.75 if below else -1.0))[:, None, :, None]
            k = 2.0 ** 30 if large else 2.0 ** -30
            for h in range(0, 128, 16):
                u[r, h:h + 16, h] = k
                if below and whole[h // 16] < 4: u[r, :, h] = k
                elif below:
                    g = (h + 16) % 128
                    u[r, g:g + 16, h] = -k
            v[r] = k * (rng.integers(0, 2, v[r].shape) * 2.0 - 1.0)
            for c in range(4): w[r, n, c, n, c] = 128.0 if below else 128.0 * (rng.integers(0, 2) * 2.0 - 1.0)
    return {"x": x.reshape(N, 128, 4 * C).astype(BF), "u": u.reshape(N, 128, 512), "v": v.astype(BF), "m": np.stack([gtable(m[r]) for r in range(N)]), **weights(rng, w.astype(BF))}
def setup_inputs_spread(rng):
    d = setup_inputs(rng)
    d["x"] = big(wide(rng, N, 128, 4 * C, cols=6))
    return d
def check_inputs(d):
    b = []
    for k, low, top in (("x", 2.0 ** -27, 2.0 ** 21), ("u", 2.0 ** -30, 2.0 ** 30), ("v", 2.0 ** -30, 2.0 ** 30)):
        a = np.abs(d[k].astype(np.float32))
        if not (np.isfinite(a).all() and ((a == 0) | (a >= low) & (a <= top)).all()): b.append("a value of " + k)
    none, least, most = [emit(mx_ref.quantize(np.full((128, 16), k, np.float32).astype(BF)))[1][0, 0] for k in (0.0, 2.0 ** -30, 2.0 ** 30)]
    for r in range(N):
        e = gentries(d["m"][r])
        if ((e < 0) | (e >= C)).any(): b.append("an entry of m")
        elif (e == np.arange(C)).any() or (at(e, e) != np.arange(C)).any(): b.append("m: no pairing")
        if ((d["wc"][r] & 0x7F) == 0x7F).any(): b.append("wc: a code that is no number")
        s = mx_ref.live(d["ws"][r])
        if ((s != none) & ((s < least) | (s > most))).any(): b.append("ws: a scale out of range")
        a = np.abs(decode(pk(d["wc"][r], d["ws"][r])).astype(np.float64)).reshape(128, 512, 4)
        if not (np.sum(a, axis=(0, 2)) <= 128).all(): b.append("W: the sizes of a column")
    return b
def reference(x, u, v, m, wc, ws):
    qu = [mx_ref.quantize(u[r]) for r in range(N)]
    lay = [pk(wc[r], ws[r]) for r in range(N)]
    now = [x[r] for r in range(N)]
    mate = [gentries(m[r]) for r in range(N)]
    j = np.arange(C)
    for h in STRIDE:
        q = [mx_ref.quantize(now[r]) for r in range(N)]
        have = [decode(q[r]).astype(BF) for r in range(N)]
        made, mates = [], []
        for r in range(N):
            e = r ^ h
            o, p = mate[r], mate[e]
            s = mx_ref.matmul(qu[r], q[r])[::16] + np.float32(0.0)
            val, low = np.maximum(s, at(s, p)), np.minimum(j, p)
            beats = (val > at(val, o)) | ((val == at(val, o)) & (low < at(low, o)))
            app = beats & at(beats, p)
            n = np.where(app, p, np.where(at(app, o), at(o, at(p, o)), o))
            one, two, slot = np.full((8, K), -1), np.full((8, K), -1), np.full((8, C), -1)
            for g in range(8):
                a = np.flatnonzero(app[g] & (j < p[g]))
                one[g, :len(a)], two[g, :len(a)] = a, p[g][a]
                slot[g, a] = np.arange(len(a))
                slot[g, p[g][a]] = np.arange(len(a))
            came = decode(mx_ref.quantize(halved(gcols(have[e], one), gcols(have[e], two)))).astype(BF)
            add = gcols(came, slot).astype(np.float32)
            own = have[r].astype(np.float32)
            z = mx_ref.quantize(halved(gcols(have[r], o), gcols(have[r], n)))
            made.append(tile([(mx_ref.matmul(pick(lay[r], np.arange(128 * b, 128 * b + 128)), z) * np.float32(0.03125) + own[:, b::4]) + add[:, b::4] for b in range(4)]))
            mates.append(n)
        now, mate = made, mates
    y, om = np.zeros((N, 128, C), np.float32), np.zeros((N, 8, C), np.float32)
    oc, osc = np.zeros((N, 128, 4 * C), np.uint8), np.zeros((N, 16, C), np.uint8)
    for r in range(N):
        q = mx_ref.quantize(now[r])
        y[r] = mx_ref.matmul(mx_ref.quantize(v[r]), q)
        om[r] = mate[r]
        oc[r], osc[r] = emit(q)
    return {"y": y, "om": om, "oc": oc, "osc": osc}

from concourse.mybir import dt, AluOpType, ActivationFunctionType

C = 384
LC = C // 16
HALF = C // 2
GW = C + 16
ROUNDS = 3
CUT = 224
TINY = 2.0 ** -117
CODES = "float8_e4m3fn_x4"


def _scratch():
    s = {
        "ps": ("psum", [128, 4096], "float32"),
        "x0": ("sbuf", [128, 4 * C], "bfloat16"),
        "ut": ("sbuf", [128, 512], "bfloat16"),
        "vt": ("sbuf", [128, 512], "bfloat16"),
        "mi": ("sbuf", [128, LC], "int32"),
        "lpi": ("sbuf", [128, LC], "int32"),
        "et": ("sbuf", [128, 2048], "bfloat16"),
        "c32": ("sbuf", [128, 128], "bfloat16"),
        "id32": ("sbuf", [128, 128], "bfloat16"),
        "gw": ("sbuf", [128, 4 * GW], "bfloat16"),
        "vi": ("sbuf", [128, LC], "int32"),
        "bi": ("sbuf", [128, LC], "int32"),
        "pi": ("sbuf", [128, 8], "int32"),
        "pf": ("sbuf", [128, 8], "float32"),
    }
    for k, n in (("w", 512), ("u", 128), ("v", 128), ("e", 512), ("z", C), ("a", C)):
        s["q" + k] = ("sbuf", [128, n], CODES)
        s["s" + k] = ("sbuf", [128, n], "uint8")
    for k in ("fh", "fm", "ga", "zt", "at", "xt"):
        s[k] = ("sbuf", [128, 4 * C], "bfloat16")
    for k in ("yo", "omr", "sc", "sc2", "val", "val2"):
        s[k] = ("sbuf", [128, C], "float32")
    for k in ("near", "far", "lowu"):
        s[k] = ("sbuf", [128, LC], "uint16")
    for k in ("place", "dif", "thr", "win", "app", "low", "win2", "app2", "low2", "orow", "oprow", "t1c", "t1o"):
        s[k] = ("sbuf", [128, C], "bfloat16")
    for k in ("yc", "yq", "t2c", "t2o"):
        s[k] = ("sbuf", [128, C + 32], "bfloat16")
    for k in ("m1", "m2", "jf", "jm", "ph", "po", "lowf", "xa", "xb", "xc", "xd", "hh"):
        s[k] = ("sbuf", [128, LC], "float32")
    for k in ("c3", "kl", "kj", "sl", "sj"):
        s[k] = ("sbuf", [128, 3 * LC], "float32")
    for r in range(ROUNDS + 1):
        s["qx%d" % r] = ("sbuf", [128, C], CODES)
        s["sx%d" % r] = ("sbuf", [128, C], "uint8")
        s["nu%d" % r] = ("sbuf", [128, LC], "uint16")
        s["kn%d" % r] = ("sbuf", [128, 3 * LC], "float32")
    for r in range(ROUNDS):
        s["lq%d" % r] = ("sbuf", [128, C], CODES)
        s["ls%d" % r] = ("sbuf", [128, C], "uint8")
        s["lp%d" % r] = ("sbuf", [128, LC], "uint16")
    return s


SCRATCH = _scratch()
SEMAPHORES = (["cv", "cs", "cp", "cg", "lm", "lx", "lu", "lw", "lv", "st", "sent"]
              + [k + str(r) for k in ("aa", "ab", "al") for r in range(ROUNDS)])


def rank_program(g, core, T, topo):
    rank = T.rank_of(core)
    if rank is None:
        return
    A = AluOpType
    F = ActivationFunctionType
    eng = {"v": g.vector, "s": g.scalar, "p": g.tensor, "y": g.sync, "g": g}
    V, S, P = g.vector, g.scalar, g.tensor

    total = {}
    known = {q: {} for q in eng}
    clock = {}
    writer = {}
    readers = {}
    serial = [0]

    def need(q, toks):
        best = {}
        for tok in toks:
            if tok[1] > best.get(tok[0], (None, 0, 0))[1]:
                best[tok[0]] = tok
        for tok in sorted(best.values(), key=lambda t: -t[2]):
            if known[q].get(tok[0], 0) >= tok[1]:
                continue
            eng[q].wait_ge(T.sem[tok[0]], tok[1])
            known[q][tok[0]] = tok[1]
            for k, n in clock.get(tok[:2], {}).items():
                if known[q].get(k, 0) < n:
                    known[q][k] = n

    def op(q, call, reads, writes, sem=None, inc=1, attach=True):
        toks = [writer[k] for k in list(reads) + list(writes)
                if k in writer and not (k[0] == "B" and writer[k][0] == "c" + q)]
        for k in writes:
            toks += readers.get(k, [])
        need(q, toks)
        name = sem or "c" + q
        ins = call()
        if attach:
            ins.then_inc(T.sem[name], inc)
        total[name] = total.get(name, 0) + inc
        serial[0] += 1
        tok = (name, total[name], serial[0])
        clock[tok[:2]] = dict(known[q])
        for k in reads:
            readers.setdefault(k, []).append(tok)
        for k in writes:
            writer[k] = tok
            readers[k] = []
        return tok

    def arrives(key, sem, n):
        serial[0] += 1
        total[sem] = n
        writer[key] = (sem, n, serial[0])

    def partner(r):
        return T.cores[rank ^ (r + 1)]

    def lanes(r):
        return len(topo.engines(core, partner(r)))

    def send(r, dst, src, sem, reads):
        to = partner(r)
        rid, pid, _ = topo.addr(to)
        op("g", lambda: g.remote_dma(dst, src, T.sem[sem], T.sem.sent, pid, rid, topo.mask(core, to)),
           reads, [], sem="sent", inc=lanes(r), attach=False)

    def bank(k, n):
        return T.ps[:, 512 * k:512 * k + n]

    def vtt(out, a, b, alu, reads, writes):
        return op("v", lambda: V.tensor_tensor(out, a, b, alu), reads, writes)

    def vts(out, a, s1, s2, o0, o1, reads, writes):
        if o1 is None:
            return op("v", lambda: V.tensor_scalar(out, a, s1, None, o0), reads, writes)
        return op("v", lambda: V.tensor_scalar(out, a, s1, s2, o0, o1), reads, writes)

    def vcopy(out, a, reads, writes):
        return op("v", lambda: V.tensor_copy(out, a), reads, writes)

    def fill(ap, c, writes):
        return op("v", lambda: V.memset(ap, c), [], writes)

    def act(out, a, scale, reads, writes):
        return op("s", lambda: S.activation(out, a, F.Copy, scale=scale), reads, writes)

    def mm(k, lq, ls, b, rq, rs, a0, a1, start, stop, reads):
        return op("p", lambda: P.matmul_mx(bank(k, a1 - a0), lq[:, 128 * b:128 * b + 128], ls[:, 128 * b:128 * b + 128],
                                           rq[:, a0:a1], rs[:, a0:a1], start, stop), reads, ["B%d" % k])

    def quant(q, s, t, a0, a1, reads, writes):
        return op("v", lambda: V.quantize_mx(q[:, a0:a1], s[:, a0:a1], t[:, 4 * a0:4 * a1]), reads, writes)

    def store(q, out, a, reads):
        return op(q, lambda: eng[q].dma_start(out, a), reads, [], sem="st", inc=16)

    four = range(4)
    for r in range(ROUNDS):
        arrives("lp%d" % r if r else "lpi", "al%d" % r, lanes(r))
        arrives("lq%da" % r, "aa%d" % r, 2 * lanes(r))
        arrives("lq%db" % r, "ab%d" % r, 2 * lanes(r))

    def send_state(r, a0, a1, tag):
        key = ["qx%d%s" % (r, tag)]
        send(r, T["lq%d" % r][:, a0:a1].bitcast(dt.uint8), T["qx%d" % r][:, a0:a1].bitcast(dt.uint8), "a%s%d" % (tag, r), key)
        send(r, T["ls%d" % r][:, a0:a1], T["sx%d" % r][:, a0:a1], "a%s%d" % (tag, r), key)

    def own_row(r):
        act(T.orow[:], T.place[:].indirect(T["nu%d" % r][:]), 1.0, ["place", "nu%d" % r], ["orow"])

    def far_row(r):
        act(T.oprow[:], T.orow[:].indirect(T["lp%d" % r][:]), 1.0, ["orow", "lp%d" % r], ["oprow"])

    def back_row(r):
        act(T.yq[:, 16:16 + C], T.oprow[:].indirect(T["nu%d" % r][:]), 0.5, ["oprow", "nu%d" % r], ["yq"])

    def least_list(r):
        p, kp = (T["lp%d" % r], "lp%d" % r) if r else (T.lpi, "lpi")
        k = T["kn%d" % r]
        return [
            lambda: vts(T.ph[:], p[:], 0.5, -0.5 * HALF, A.mult, A.add, [kp], ["ph"]),
            lambda: vtt(T.lowf[:], T.ph[:], T.jm[:], A.min, ["ph", "jm"], ["lowf"]),
            lambda: vts(T.lowu[:], T.lowf[:], 2.0, float(HALF), A.mult, A.add, ["lowf"], ["lowu"]),
            lambda: vtt(T.po[:], T.ph[:], k[:, 2::3], A.subtract, ["ph", "kn%d2" % r], ["po"]),
        ]

    def far_terms():
        for i, sign in ((0, 1.0), (1, -1.0)):
            op("s", lambda: S.activation(T.kl[:, i::3], T.ph[:], F.Identity, bias=sign * 0.5 * (HALF - C), scale=sign),
               ["ph"], ["kl%d" % i])

    def least_row():
        act(T.low[:], T.place[:].indirect(T.lowu[:]), TINY, ["place", "lowu"], ["low"])

    def ties(r):
        vtt(T.thr[:], T.low[:].indirect(T["nu%d" % r][:]), T.low2[:], A.subtract, ["low", "low2", "nu%d" % r], ["thr"])

    def to_list(y, t1, t2, xa, xb):
        return [
            lambda: op("v", lambda: V.transpose(T[t1][:], T[y][:, 16:16 + C]), [y, "pads"], [t1]),
            lambda: op("v", lambda: V.transpose(T[t2][:], T[y][:]), [y, "pads"], [t2]),
            lambda: vtt(T[xa][:], T[t1][:, 0:C:16], T.m1[:], A.mult, [t1, "m1"], [xa]),
            lambda: vtt(T[xb][:], T[t2][:, 16:16 + C:16], T.m2[:], A.mult, [t2, "m2"], [xb]),
        ]

    def terms(r):
        k = T["kn%d" % r]
        return to_list("yq", "t1o", "t2o", "xc", "xd") + [
            lambda: vtt(T.hh[:], T.xc[:], T.xd[:], A.add, ["xc", "xd"], ["hh"]),
            lambda: vtt(k[:, 1::3], T.hh[:], T.ph[:], A.subtract, ["hh", "ph"], ["kn%d1" % r]),
            lambda: vtt(k[:, 0::3], T.hh[:], T.po[:], A.add, ["hh", "po"], ["kn%d0" % r]),
        ]

    def scores(r, k, a0, a1, key):
        mm(k, T.qu, T.su, 0, T["qx%d" % r], T["sx%d" % r], a0, a1, True, True, key + ["qu"])

    def score_rows(k, a0, a1, tag):
        act(T.sc[:, a0:a1], bank(k, a1 - a0), 1.0, [], ["B%d" % k, "sc" + tag])
        act(T.sc2[:, a0:a1], bank(k, a1 - a0), 1.0, [], ["B%d" % k, "sd" + tag])

    op("y", lambda: g.sync.dma_start(T.mi[:], T.m[:]), [], ["mi"], sem="lm", inc=16)
    op("y", lambda: g.sync.dma_start(T.ut[:], T.u[:]), [], ["ut"], sem="lu", inc=16)
    op("y", lambda: g.sync.dma_start(T.x0[:], T.x[:]), [], ["x0"], sem="lx", inc=16)
    op("y", lambda: g.sync.dma_start(T.qw[:].bitcast(dt.uint8), T.wc[:]), [], ["qw0"], sem="lw", inc=16)
    op("y", lambda: g.sync.dma_start(T.sw[:], T.ws[:]), [], ["qw"], sem="lw", inc=16)
    op("y", lambda: g.sync.dma_start(T.vt[:], T.v[:]), [], ["vt"], sem="lv", inc=16)

    fill(T.c32[:], 32.0, ["c32"])
    op("g", lambda: g.iota(T.vi[:], [[16, LC]], 0, 1), [], ["vi"])
    op("g", lambda: g.affine_select(T.id32[:], T.c32[:], [[-1, 128]], A.is_equal, 0.0, 0, 1), ["c32"], ["id32"])
    op("g", lambda: g.iota(T.place[:], [[1, C]], -HALF, 0, allow_small_or_imprecise_dtypes=True), [], ["place"])
    send(0, T.lpi[:], T.mi[:], "al0", ["mi"])
    fill(T.et[:], 0.0, ["et%d" % b for b in four])
    vts(T.bi[:], T.vi[:], 4, 1, A.arith_shift_right, A.bitwise_and, ["vi"], ["bi"])
    vts(T.pi[:, 0:1], T.vi[:, 0:1], 128 - 16, None, A.bitwise_and, None, ["vi"], ["pi"])
    for b in four:
        vcopy(T.et[:, 512 * b + b:512 * b + 512:4], T.id32[:], ["id32"], ["et%d" % b])
    vcopy(T.nu0[:], T.mi[:], ["mi"], ["nu0"])
    vcopy(T.pf[:, 0:1], T.pi[:, 0:1], ["pi"], ["pf"])
    quant(T.qe, T.se, T.et, 0, 512, ["et%d" % b for b in four], ["qe"])
    own_row(0)
    vts(T.jf[:], T.vi[:], T.pf[:, 0:1], None, A.subtract, None, ["vi", "pf"], ["jf"])
    vts(T.kn0[:, 2::3], T.mi[:], -float(HALF), None, A.add, None, ["mi"], ["kn02"])
    vts(T.jm[:], T.jf[:], 0.5, -0.5 * HALF, A.mult, A.add, ["jf"], ["jm"])
    quant(T.qu, T.su, T.ut, 0, 128, ["ut"], ["qu"])
    quant(T.qx0, T.sx0, T.x0, 0, C, ["x0"], ["qx0a", "qx0b"])
    send_state(0, 0, CUT, "a")
    send_state(0, CUT, C, "b")
    scores(0, 4, 0, C, ["qx0a", "qx0b"])
    vcopy(T.m2[:], T.bi[:], ["bi"], ["m2"])
    vts(T.m1[:], T.bi[:], -1.0, 1.0, A.mult, A.add, ["bi"], ["m1"])
    for k in ("yc", "yq"):
        fill(T[k][:, 0:16], 0.0, [k + "0"])
        fill(T[k][:, 16 + C:32 + C], 0.0, [k + "1"])
    fill(T.c3[:, 0::3], 0.0, ["c30"])
    fill(T.kl[:, 2::3], float(C), ["kl2"])
    fill(T.kj[:, 2::3], float(C), ["kj2"])
    act(T.sc[:], bank(4, C), 1.0, [], ["B4", "sca", "scb"])
    act(T.sc2[:], bank(4, C), 1.0, [], ["B4", "sda", "sdb"])

    for r in range(ROUNDS):
        last = r == ROUNDS - 1
        qx, sx, lq, ls = T["qx%d" % r], T["sx%d" % r], T["lq%d" % r], T["ls%d" % r]
        qn, sn = T["qx%d" % (r + 1)], T["sx%d" % (r + 1)]
        o, p, n = T["nu%d" % r], T["lp%d" % r], T["nu%d" % (r + 1)]
        ko, kp, kn = "nu%d" % r, "lp%d" % r, "nu%d" % (r + 1)
        kx = ["qx%da" % r, "qx%db" % r]
        kxn = ["qx%da" % (r + 1), "qx%db" % (r + 1)]

        def halve(b):
            act(T.fh[:, C * b:C * b + C], bank(b, C), 1.0 / 64, [], ["B%d" % b, "fh%d" % b])

        def edge_values():
            vtt(T.val[:], T.sc[:].indirect(p[:]), T.sc2[:], A.max, ["sca", "scb", "sda", "sdb", kp], ["val"])

        def second(name):
            vcopy(T[name + "2"][:], T[name][:], [name], [name + "2"])

        for b in four:
            mm(b, T.qe, T.se, b, qx, sx, 0, C, True, True, kx + ["qe"])
        ahead = terms(r)
        if r == 0:
            vcopy(T.lp0[:], T.lpi[:], ["lpi"], ["lp0"])
            small = least_list(0)
            for call in small[0:3]:
                call()
            halve(0)
            far_terms()
            least_row()
            edge_values()
            small[3]()
            act(T.val2[:], T.val[:], 1.0, ["val"], ["val2"])
            far_row(0)
            back_row(0)
            second("low")
            rest = [lambda: vts(T.kj[:, 0::3], T.jf[:], 0.5, -0.5 * C, A.mult, A.add, ["jf"], ["kj0"]),
                    lambda: vts(T.kj[:, 1::3], T.jf[:], -0.5, 0.5 * C, A.mult, A.add, ["jf"], ["kj1"])]
            rest += [lambda b=b: fill(T.gw[:, GW * b + C:GW * b + GW], 0.0, ["gz%d" % b]) for b in four]
            rest.pop(0)()
            ties(0)
            for b in range(1, 4):
                halve(b)
            slots = [rest[0:1], rest[1:3], rest[3:5], ahead[0:2], ahead[2:4], ahead[4:5], ahead[5:7]]
        else:
            back_row(r)
            edge_values()
            act(T.val2[:], T.val[:], 1.0, ["val"], ["val2"])
            for b in four:
                halve(b)
            for call in ahead[0:3]:
                call()
            slots = [ahead[3:4], ahead[4:5], ahead[5:6], ahead[6:7], [], [], []]
        writer["pads"] = max((writer[k] for k in ("yc0", "yc1", "yq0", "yq1")), key=lambda t: t[1])
        for b in four:
            mm(b, T.qe, T.se, b, qx, sx, 0, CUT, True, False, kx + ["qe"])
        for b in four:
            act(T.fm[:, C * b:C * b + C], T.fh[:, C * b:C * b + C].indirect(o[:]), 1.0, ["fh%d" % b, ko], ["fm%d" % b])

        chain = [
            lambda: vtt(T.dif[:], T.val[:].indirect(o[:]), T.val2[:], A.subtract, ["val", "val2", ko], ["dif"]),
            lambda: vtt(T.win[:], T.dif[:], T.thr[:], A.is_lt, ["dif", "thr"], ["win"]),
            lambda: second("win"),
            lambda: vtt(T.app[:], T.win[:].indirect(p[:]), T.win2[:], A.min, ["win", "win2", kp], ["app"]),
            lambda: second("app"),
            lambda: vtt(T.yc[:, 16:16 + C], T.app[:].indirect(o[:]), T.app2[:], A.subtract, ["app", "app2", ko], ["yc"]),
        ]
        for call, between in zip(chain, slots):
            call()
            for other in between:
                other()
        turn = to_list("yc", "t1c", "t2c", "xa", "xb")
        for call in turn:
            call()
        for other in slots[6]:
            other()
        vtt(T.c3[:, 1::3], T.xa[:], T.xb[:], A.add, ["xa", "xb"], ["c31"])
        vtt(T.c3[:, 2::3], T.xa[:], T.xb[:], A.add, ["xa", "xb"], ["c32k"])
        kc = ["c30", "c31", "c32k"]
        knext = T["kn%d" % (r + 1)]
        op("v", lambda: V.tensor_tensor_scan(knext[:], T.c3[:], T["kn%d" % r][:], 0.0, A.mult, A.add),
           kc + ["kn%d%d" % (r, i) for i in range(3)], ["kn%d%d" % (r + 1, i) for i in range(3)])
        op("v", lambda: V.tensor_tensor_scan(T.sj[:], T.c3[:], T.kj[:], 0.0, A.mult, A.add), kc + ["kj0", "kj1", "kj2"], ["sj"])
        vts(n[:], knext[:, 2::3], float(HALF), None, A.add, None, ["kn%d2" % (r + 1)], [kn])
        op("v", lambda: V.tensor_tensor_scan(T.sl[:], T.c3[:], T.kl[:], 0.0, A.mult, A.add), kc + ["kl0", "kl1", "kl2"], ["sl"])
        vcopy(T.near[:], T.sj[:, 2::3], ["sj"], ["near"])
        if not last:
            send(r + 1, T["lp%d" % (r + 1)][:], n[:], "al%d" % (r + 1), [kn])

        for a0, a1, tag in ((0, CUT, "a"), (CUT, C, "b")):
            for b in four:
                mm(4 + b, T.qe, T.se, b, lq, ls, a0, a1, True, True, ["lq%d%s" % (r, tag), "qe"])
            if tag == "b" and not last:
                own_row(r + 1)
            for b in four:
                act(T.gw[:, GW * b + a0:GW * b + a1], bank(4 + b, a1 - a0), 1.0 / 64, [], ["B%d" % (4 + b), "gp%d" % b])
        for b in four:
            act(T.ga[:, C * b:C * b + C], T.gw[:, GW * b:GW * b + GW].indirect(T.near[:]), 1.0,
                ["gp%d" % b, "gz%d" % b, "near"], ["ga%d" % b])

        for b in four:
            vtt(T.zt[:, b:4 * C:4], T.fh[:, C * b:C * b + C].indirect(n[:]), T.fm[:, C * b:C * b + C], A.add,
                ["fh%d" % b, "fm%d" % b, kn], ["zt%d" % b])
        vcopy(T.far[:], T.sl[:, 2::3], ["sl"], ["far"])
        quant(T.qz, T.sz, T.zt, 0, C, ["zt%d" % b for b in four], ["qz"])
        for b in four:
            mm(b, T.qw, T.sw, b, T.qz, T.sz, 0, CUT, False, False, ["qz", "qw"])
        for b in four:
            mm(4 + b, T.qe, T.se, b, qx, sx, CUT, C, True, False, kx + ["qe"])
        for b in four:
            mm(4 + b, T.qw, T.sw, b, T.qz, T.sz, CUT, C, False, False, ["qz", "qw"])
        if last:
            op("s", lambda: S.activation(T.omr[:], T.place[:].indirect(n[:]), F.Identity, bias=float(HALF)),
               ["place", kn], ["omr"])
            store("y", T.om[:], T.omr[0:128:16, :], ["omr"])
            small = [lambda: quant(T.qv, T.sv, T.vt, 0, 128, ["vt"], ["qv"])]
            slots = [[], [], [], small]
        else:
            far_row(r + 1)
            small = least_list(r + 1)
            slots = [small[0:1], small[1:2], small[2:3], small[3:4]]

        def pairs(i, b, a0, a1):
            vtt(T.at[:, 4 * a0 + b:4 * a1:4], T.gw[:, GW * b:GW * b + GW].indirect(T.far[:, a0 // 16:a1 // 16]),
                T.ga[:, C * b + a0:C * b + a1], A.add, ["gp%d" % b, "gz%d" % b, "ga%d" % b, "far"], ["at%d%d" % (i, b)])

        def finish(i, a0, a1):
            quant(T.qa, T.sa, T.at, a0, a1, ["at%d%d" % (i, b) for b in four], ["qa%d" % i])
            for b in four:
                mm(4 * i + b, T.qe, T.se, b, T.qa, T.sa, a0, a1, False, True, ["qa%d" % i, "qe"])

        for b in four:
            pairs(0, b, 0, CUT)
            for call in slots[b]:
                call()
        if not last:
            far_terms()
            least_row()
        finish(0, 0, CUT)
        for b in four:
            act(T.xt[:, b:4 * CUT:4], bank(b, CUT), 1.0 / 32, [], ["B%d" % b, "xt0%d" % b])
        for b in four:
            pairs(1, b, CUT, C)
        finish(1, CUT, C)
        if not last:
            act(T.low2[:], T.low[:], 1.0, ["low"], ["low2"])
        quant(qn, sn, T.xt, 0, CUT, ["xt0%d" % b for b in four], [kxn[0]])
        if last:
            store("y", T.oc[:, 0:4 * CUT], qn[:, 0:CUT].bitcast(dt.uint8), [kxn[0]])
            mm(0, T.qv, T.sv, 0, qn, sn, 0, CUT, True, True, [kxn[0], "qv"])
        else:
            send_state(r + 1, 0, CUT, "a")
            scores(r + 1, 0, 0, CUT, [kxn[0]])
        for b in four:
            view = T.xt[:, 4 * CUT + b:4 * C:4]
            if b < 2:
                act(view, bank(4 + b, C - CUT), 1.0 / 32, [], ["B%d" % (4 + b), "xt1%d" % b])
            else:
                vts(view, bank(4 + b, C - CUT), 1.0 / 32, None, A.mult, None, [], ["B%d" % (4 + b), "xt1%d" % b])
        quant(qn, sn, T.xt, CUT, C, ["xt1%d" % b for b in four], [kxn[1]])
        if last:
            mm(1, T.qv, T.sv, 0, qn, sn, CUT, C, True, True, [kxn[1], "qv"])
            act(T.yo[:, 0:CUT], bank(0, CUT), 1.0, [], ["B0", "y0"])
            store("y", T.y[:, 0:CUT], T.yo[:, 0:CUT], ["y0"])
            act(T.yo[:, CUT:C], bank(1, C - CUT), 1.0, [], ["B1", "y1"])
            store("y", T.oc[:, 4 * CUT:4 * C], qn[:, CUT:C].bitcast(dt.uint8), [kxn[1]])
            for k in four:
                store("y", T.osc[4 * k:4 * k + 4, :], sn[32 * k:32 * k + 4, :], kxn)
            store("s", T.y[:, CUT:C], T.yo[:, CUT:C], ["y1"])
        else:
            score_rows(0, 0, CUT, "a")
            scores(r + 1, 4, CUT, C, [kxn[1]])
            score_rows(4, CUT, C, "b")
            send_state(r + 1, CUT, C, "b")
            ties(r + 1)

    for name, n in total.items():
        if known["g"].get(name, 0) < n:
            g.wait_ge(T.sem[name], n)
